import numpy as np
import ml_dtypes


def mxq(x, axis, fmt="e4m3"):
    dtype, down = {"e4m3": (ml_dtypes.float8_e4m3fn, 7), "e5m2": (ml_dtypes.float8_e5m2, 14)}[fmt]
    v = np.moveaxis(np.asarray(x, np.float32).astype(ml_dtypes.bfloat16).astype(np.float64), axis, -1)
    blocks = v.reshape(v.shape[:-1] + (-1, 32))
    amax = np.abs(blocks).max(-1, keepdims=True)
    byte = np.maximum(np.where(amax > 0, np.frexp(amax)[1] - 1 + 127, 0) - down, 1)
    scale = np.exp2(byte - 127.0)
    codes = (blocks / scale).astype(np.float32).astype(dtype).astype(np.float64)
    return np.moveaxis((codes * scale).reshape(v.shape), -1, axis)


WIDE = False


def mx_kscale(k):
    if not WIDE:
        return np.ones(k)
    levels = np.array([10, -10, 5, -5, 0])
    if k % 512:
        return np.exp2(np.random.permutation(np.resize(levels, k // 32))).repeat(32)
    a = np.empty((k // 512, 16))
    for p in range(k // 512):
        a[p, :8] = np.random.permutation(np.resize(levels, 8))
        for g in range(8):
            far = levels[np.abs(levels - a[p, g]) >= 10]
            a[p, g + 8] = far[np.random.randint(len(far))]
    return np.exp2(a.ravel()).repeat(32)


def f64(x):
    return np.asarray(x).astype(np.float64)


def striped(idx):
    return np.tile(idx.reshape(-1, 16).T, (8, 1)).astype(np.uint16)


def unstriped(offs):
    return offs[:16].T.reshape(-1).astype(np.int64)


def relu(v):
    return np.maximum(v, 0.0)


K, T, E, C, H, N = 512, 768, 2, 256, 1024, 384


def by_expert(wq, xq):
    return np.concatenate([wq[e].T @ xq[:, e * C:(e + 1) * C] for e in range(E)], axis=1)


def setup_inputs():
    n = np.random.standard_normal
    s = mx_kscale(K)[:, None]
    u = mx_kscale(H)
    return {
        "xT": (n((K, T)) * s).astype(np.float32),
        "w1": (n((E, K, H)) / np.sqrt(K) / s[None] * u[None, None, :]).astype(np.float32),
        "w2": (n((E, H, N)) / np.sqrt(H) / u[None, :, None]).astype(np.float32),
        "gate": np.tile(np.random.uniform(0.2, 1.0, E * C), (N, 1)).astype(np.float32),
        "offs": striped(np.random.permutation(T)[:E * C]),
    }


def reference(xT, w1, w2, gate, offs):
    idx = unstriped(offs)
    xq = mxq(f64(xT)[:, idx], 0, "e4m3")
    h = relu(by_expert(mxq(f64(w1), 1, "e4m3"), xq))
    y = by_expert(mxq(f64(w2), 1, "e4m3"), mxq(h, 0, "e4m3"))
    out = np.zeros((N, T))
    out[:, idx] = f64(gate) * y
    return out

@@ -1,0 +1,162 @@
+from contextlib import ExitStack
+
+import concourse.mybir as mybir
+
+K, T, E, C, H, N = 512, 768, 2, 256, 1024, 384
+SLOTS = E * C
+P = 128
+PACK = 4
+HPASS = H // 512
+NB = N // P
+HALF = C // 2
+
+F32 = mybir.dt.float32
+BF16 = mybir.dt.bfloat16
+U32 = mybir.dt.uint32
+U16 = mybir.dt.uint16
+U8 = mybir.dt.uint8
+FP8X4 = mybir.dt.float8_e4m3fn_x4
+RELU = mybir.ActivationFunctionType.Relu
+MULT = mybir.AluOpType.mult
+
+FLOPS = 2 * SLOTS * (K * H + H * N)
+BYTES = 4 * (K * T + E * K * H + E * H * N + SLOTS + N * T) + 2 * SLOTS
+
+
+def interleave(nc, grouped, raw, width, scalar_cols):
+    def piece(copy, lo, hi):
+        copy(
+            out=grouped[:, lo:hi, :].rearrange("p (c i) t -> p c t i", i=4),
+            in_=raw[:, :, lo:hi].rearrange("p t (c i) -> p c t i", i=4),
+        )
+    if scalar_cols > 0:
+        piece(nc.scalar.copy, 0, scalar_cols)
+    if scalar_cols < width:
+        piece(nc.vector.tensor_copy, scalar_cols, width)
+
+
+def interleave_permuted(nc, grouped, raw, scalar_ms):
+    def piece(copy, lo, hi):
+        copy(
+            out=grouped[:, :, lo:hi, :].rearrange("p t m j -> p m j t"),
+            in_=raw[:, :, 4 * lo:4 * hi].rearrange("p j (m t) -> p m j t", t=4),
+        )
+    if scalar_ms > 0:
+        piece(nc.scalar.copy, 0, scalar_ms)
+    if scalar_ms < P:
+        piece(nc.vector.tensor_copy, scalar_ms, P)
+
+
+def tile_routed_moe_kernel(tc, xT, w1, w2, gate, offs, out):
+    nc = tc.nc
+    with ExitStack() as ctx:
+        keep = ctx.enter_context(tc.tile_pool(name="keep", bufs=1))
+        hpsum = ctx.enter_context(tc.psum_pool(name="hpsum", bufs=4))
+        ypsum = ctx.enter_context(tc.psum_pool(name="ypsum", bufs=4))
+
+        offsets = keep.tile([P, SLOTS // 16], U16, name="offsets")
+
+        x_cuts = [(0, 512), (512, 768)]
+        x_view = xT.rearrange("(p t) n -> p t n", t=PACK)
+        x_raw = []
+        for i, (lo, hi) in enumerate(x_cuts):
+            raw = keep.tile([P, PACK, hi - lo], F32, name=f"x_raw{i}")
+            nc.sync.dma_start(out=raw[:], in_=x_view[:, :, lo:hi])
+            x_raw.append(raw)
+            if i == 0:
+                nc.sync.dma_start(offsets[:], offs)
+        gate_sb = keep.tile([P, SLOTS], F32, name="gate_sb")
+        w1_raw, w2_raw = {}, {}
+        for e in range(E):
+            for g in range(HPASS):
+                raw = keep.tile([P, PACK, 512], F32, name=f"w1_raw{e}{g}")
+                nc.sync.dma_start(out=raw[:], in_=w1[e].rearrange("(p j) c -> p j c", j=PACK)[:, :, g * 512:(g + 1) * 512])
+                w1_raw[e, g] = raw
+            if e == 0:
+                nc.sync.dma_start(out=gate_sb[:], in_=gate[0:P, :])
+            for g in range(HPASS):
+                raw = keep.tile([P, PACK, N], F32, name=f"w2_raw{e}{g}")
+                nc.sync.dma_start(out=raw[:], in_=w2[e, g * 512:(g + 1) * 512, :].rearrange("(p t) n -> p t n", t=PACK))
+                w2_raw[e, g] = raw
+
+        windows = []
+        for b in range(NB):
+            window = keep.tile([P, T], F32, name=f"window{b}")
+            nc.vector.memset(window[:], 0.0)
+            windows.append(window)
+
+        x_words = keep.tile([P, T], U32, name="x_words", align_bytes=64)
+        x_scales = keep.tile([P, T], U8, name="x_scales", align_bytes=64)
+        nc.gpsimd.memset(x_scales[:], 0)
+        x_grouped = keep.tile([P, T, PACK], BF16, name="x_grouped", align_bytes=64)
+        for i, (lo, hi) in enumerate(x_cuts):
+            interleave(nc, x_grouped[:, lo:hi, :], x_raw[i], hi - lo, (hi - lo) // 3 // 4 * 4)
+            nc.vector.quantize_mx(
+                out=x_words[:, lo:hi].bitcast(FP8X4),
+                scales=x_scales[:, lo:hi],
+                in_=x_grouped[:, lo:hi, :].rearrange("p n t -> p (n t)"),
+            )
+
+        w1_scalar = {0: 88, 1: 104}
+        w2_scalar = {0: 256, 1: 256}
+        for e in range(E):
+            columns = offsets[:, e * C // 16:(e + 1) * C // 16]
+            g_words = keep.tile([P, C], U32, name=f"g_words{e}", align_bytes=64)
+            g_scales = keep.tile([P, C], U8, name=f"g_scales{e}", align_bytes=64)
+            nc.vector.tensor_copy(out=g_words[:], in_=x_words[:].indirect(columns))
+            nc.vector.tensor_copy(out=g_scales[:], in_=x_scales[:].indirect(columns))
+
+            h_words = keep.tile([P, HPASS, C], U32, name=f"h_words{e}", align_bytes=64)
+            h_scales = keep.tile([P, HPASS, C], U8, name=f"h_scales{e}", align_bytes=64)
+            for g in range(HPASS):
+                w_grouped = keep.tile([P, PACK, P, PACK], BF16, name=f"w1_grouped{e}{g}", align_bytes=64)
+                interleave_permuted(nc, w_grouped, w1_raw[e, g], w1_scalar[e])
+                w_words = keep.tile([P, 512], U32, name=f"w1_words{e}{g}", align_bytes=64)
+                w_scales = keep.tile([P, 512], U8, name=f"w1_scales{e}{g}", align_bytes=64)
+                nc.vector.quantize_mx(
+                    out=w_words[:].bitcast(FP8X4), scales=w_scales[:],
+                    in_=w_grouped[:].rearrange("p t m j -> p (t m j)"),
+                )
+                for s in range(C // HALF):
+                    cols = slice(s * HALF, (s + 1) * HALF)
+                    bank = hpsum.tile([P, PACK, HALF], F32, name="h_bank")
+                    for t in range(PACK):
+                        chan = slice(t * P, (t + 1) * P)
+                        nc.tensor.matmul_mx(
+                            out=bank[:, t, :],
+                            lhsT=w_words[:, chan].bitcast(FP8X4), lhsT_scale=w_scales[:, chan],
+                            rhs=g_words[:, cols].bitcast(FP8X4), rhs_scale=g_scales[:, cols],
+                            start=True, stop=True,
+                        )
+                    h_grouped = keep.tile([P, HALF, PACK], BF16, name=f"h_grouped{e}{g}{s}", align_bytes=64)
+                    nc.scalar.activation(out=h_grouped[:], in_=bank[:].rearrange("p t n -> p n t"), func=RELU)
+                    nc.vector.quantize_mx(
+                        out=h_words[:, g, cols].bitcast(FP8X4), scales=h_scales[:, g, cols],
+                        in_=h_grouped[:].rearrange("p n t -> p (n t)"),
+                    )
+
+            w2_words = keep.tile([P, HPASS, N], U32, name=f"w2_words{e}", align_bytes=64)
+            w2_scales = keep.tile([P, HPASS, N], U8, name=f"w2_scales{e}", align_bytes=64)
+            for g in range(HPASS):
+                w_grouped = keep.tile([P, N, PACK], BF16, name=f"w2_grouped{e}{g}", align_bytes=64)
+                interleave(nc, w_grouped, w2_raw[e, g], N, w2_scalar[e])
+                for lo, hi in ((0, 256), (256, 384)):
+                    nc.vector.quantize_mx(
+                        out=w2_words[:, g, lo:hi].bitcast(FP8X4), scales=w2_scales[:, g, lo:hi],
+                        in_=w_grouped[:, lo:hi, :].rearrange("p n t -> p (n t)"),
+                    )
+            for b in range(NB):
+                feat = slice(b * P, (b + 1) * P)
+                bank = ypsum.tile([P, C], F32, name="y_bank")
+                for g in range(HPASS):
+                    nc.tensor.matmul_mx(
+                        out=bank[:],
+                        lhsT=w2_words[:, g, feat].bitcast(FP8X4), lhsT_scale=w2_scales[:, g, feat],
+                        rhs=h_words[:, g, :].bitcast(FP8X4), rhs_scale=h_scales[:, g, :],
+                        start=(g == 0), stop=(g == HPASS - 1),
+                    )
+                y = keep.tile([P, C], F32, name=f"y{e}{b}")
+                nc.vector.tensor_tensor(y[:], bank[:], gate_sb[:, e * C:(e + 1) * C], MULT)
+                nc.vector.tensor_copy(windows[b][:].indirect(columns), y[:])
+                if e == E - 1:
+                    nc.sync.dma_start(out=out[feat, :], in_=windows[b][:])

@@ -23,61 +23,66 @@ FLOPS = 2 * SLOTS * (K * H + H * N)
 BYTES = 4 * (K * T + E * K * H + E * H * N + SLOTS + N * T) + 2 * SLOTS
 
 
-def interleave(nc, grouped, raw, width, scalar_cols):
-    def piece(copy, lo, hi):
-        copy(
-            out=grouped[:, lo:hi, :].rearrange("p (c i) t -> p c t i", i=4),
-            in_=raw[:, :, lo:hi].rearrange("p t (c i) -> p c t i", i=4),
-        )
-    if scalar_cols > 0:
-        piece(nc.scalar.copy, 0, scalar_cols)
-    if scalar_cols < width:
-        piece(nc.vector.tensor_copy, scalar_cols, width)
+def interleave(copy, grouped, raw, lo, hi):
+    copy(
+        out=grouped[:, lo:hi, :].rearrange("p (c i) t -> p c t i", i=4),
+        in_=raw[:, :, lo:hi].rearrange("p t (c i) -> p c t i", i=4),
+    )
 
 
-def interleave_permuted(nc, grouped, raw, scalar_ms):
-    def piece(copy, lo, hi):
-        copy(
-            out=grouped[:, :, lo:hi, :].rearrange("p t m j -> p m j t"),
-            in_=raw[:, :, 4 * lo:4 * hi].rearrange("p j (m t) -> p m j t", t=4),
-        )
-    if scalar_ms > 0:
-        piece(nc.scalar.copy, 0, scalar_ms)
-    if scalar_ms < P:
-        piece(nc.vector.tensor_copy, scalar_ms, P)
+def interleave_permuted(copy, grouped, raw, lo, hi):
+    copy(
+        out=grouped[:, :, lo:hi, :].rearrange("p t m j -> p m j t"),
+        in_=raw[:, :, 4 * lo:4 * hi].rearrange("p j (m t) -> p m j t", t=4),
+    )
 
 
 def tile_routed_moe_kernel(tc, xT, w1, w2, gate, offs, out):
     nc = tc.nc
     with ExitStack() as ctx:
         keep = ctx.enter_context(tc.tile_pool(name="keep", bufs=1))
+        ring = ctx.enter_context(tc.tile_pool(name="ring", bufs=3))
         hpsum = ctx.enter_context(tc.psum_pool(name="hpsum", bufs=4))
         ypsum = ctx.enter_context(tc.psum_pool(name="ypsum", bufs=4))
-
+        on = {"S": nc.scalar.copy, "V": nc.vector.tensor_copy}
         offsets = keep.tile([P, SLOTS // 16], U16, name="offsets")
-
-        x_cuts = [(0, 512), (512, 768)]
         x_view = xT.rearrange("(p t) n -> p t n", t=PACK)
-        x_raw = []
-        for i, (lo, hi) in enumerate(x_cuts):
-            raw = keep.tile([P, PACK, hi - lo], F32, name=f"x_raw{i}")
-            nc.sync.dma_start(out=raw[:], in_=x_view[:, :, lo:hi])
-            x_raw.append(raw)
-            if i == 0:
-                nc.sync.dma_start(offsets[:], offs)
+        x_cuts = ((0, 512), (512, 768))
+        x_raw, w1_raw, w2_raw = {}, {}, {}
         gate_sb = keep.tile([P, SLOTS], F32, name="gate_sb")
-        w1_raw, w2_raw = {}, {}
-        for e in range(E):
-            for g in range(HPASS):
-                raw = keep.tile([P, PACK, 512], F32, name=f"w1_raw{e}{g}")
+        loads = ["X0","o","X1","A00","A01","g","B00","B01","A10","A11","B10","B11"]
+        ring_loads = [name for name in loads if name[0] in "AB"]
+        waiting = list(loads)
+
+        def issue(name):
+            if name[0] == "X":
+                i = int(name[1])
+                lo, hi = x_cuts[i]
+                raw = keep.tile([P, PACK, hi - lo], F32, name=f"x_raw{i}")
+                nc.sync.dma_start(out=raw[:], in_=x_view[:, :, lo:hi])
+                x_raw[i] = raw
+            elif name == "o":
+                nc.sync.dma_start(offsets[:], offs)
+            elif name == "g":
+                nc.sync.dma_start(out=gate_sb[:], in_=gate[0:P, :])
+            elif name[0] == "A":
+                e, g = int(name[1]), int(name[2])
+                raw = ring.tile([P, PACK, 512], F32, name="w_raw")
                 nc.sync.dma_start(out=raw[:], in_=w1[e].rearrange("(p j) c -> p j c", j=PACK)[:, :, g * 512:(g + 1) * 512])
                 w1_raw[e, g] = raw
-            if e == 0:
-                nc.sync.dma_start(out=gate_sb[:], in_=gate[0:P, :])
-            for g in range(HPASS):
-                raw = keep.tile([P, PACK, N], F32, name=f"w2_raw{e}{g}")
+            else:
+                e, g = int(name[1]), int(name[2])
+                raw = ring.tile([P, PACK, N], F32, name="w_raw")
                 nc.sync.dma_start(out=raw[:], in_=w2[e, g * 512:(g + 1) * 512, :].rearrange("(p t) n -> p t n", t=PACK))
                 w2_raw[e, g] = raw
+
+        def issue_through(k):
+            if k < len(ring_loads):
+                while ring_loads[k] in waiting:
+                    issue(waiting.pop(0))
+
+        while waiting and (waiting[0] not in ring_loads or ring_loads.index(waiting[0]) < 3):
+            issue(waiting.pop(0))
 
         windows = []
         for b in range(NB):
@@ -89,74 +94,121 @@ def tile_routed_moe_kernel(tc, xT, w1, w2, gate, offs, out):
         x_scales = keep.tile([P, T], U8, name="x_scales", align_bytes=64)
         nc.gpsimd.memset(x_scales[:], 0)
         x_grouped = keep.tile([P, T, PACK], BF16, name="x_grouped", align_bytes=64)
-        for i, (lo, hi) in enumerate(x_cuts):
-            interleave(nc, x_grouped[:, lo:hi, :], x_raw[i], hi - lo, (hi - lo) // 3 // 4 * 4)
-            nc.vector.quantize_mx(
-                out=x_words[:, lo:hi].bitcast(FP8X4),
-                scales=x_scales[:, lo:hi],
-                in_=x_grouped[:, lo:hi, :].rearrange("p n t -> p (n t)"),
-            )
-
-        w1_scalar = {0: 88, 1: 104}
-        w2_scalar = {0: 256, 1: 256}
+        x_shares = [104,32]
+        w1_shares = [[128,128],[128,128]]
+        w2_shares = [[384,128],[128,128]]
+        h_engines = ["SVSV","SSSS"]
+        y_engines = ["VVS","SSS"]
+        words1, scales1, grouped1, h_grouped, grouped2, sums = {}, {}, {}, {}, {}, {}
+        g_words, g_scales, h_words, h_scales, words2, scales2 = {}, {}, {}, {}, {}, {}
+        done = set()
         for e in range(E):
-            columns = offsets[:, e * C // 16:(e + 1) * C // 16]
-            g_words = keep.tile([P, C], U32, name=f"g_words{e}", align_bytes=64)
-            g_scales = keep.tile([P, C], U8, name=f"g_scales{e}", align_bytes=64)
-            nc.vector.tensor_copy(out=g_words[:], in_=x_words[:].indirect(columns))
-            nc.vector.tensor_copy(out=g_scales[:], in_=x_scales[:].indirect(columns))
+            for table, shape, dtype, label in (
+                (g_words, [P, C], U32, "g_words"), (g_scales, [P, C], U8, "g_scales"),
+                (h_words, [P, HPASS, C], U32, "h_words"), (h_scales, [P, HPASS, C], U8, "h_scales"),
+                (words2, [P, HPASS, N], U32, "w2_words"), (scales2, [P, HPASS, N], U8, "w2_scales"),
+            ):
+                table[e] = keep.tile(shape, dtype, name=f"{label}{e}", align_bytes=64)
 
-            h_words = keep.tile([P, HPASS, C], U32, name=f"h_words{e}", align_bytes=64)
-            h_scales = keep.tile([P, HPASS, C], U8, name=f"h_scales{e}", align_bytes=64)
-            for g in range(HPASS):
-                w_grouped = keep.tile([P, PACK, P, PACK], BF16, name=f"w1_grouped{e}{g}", align_bytes=64)
-                interleave_permuted(nc, w_grouped, w1_raw[e, g], w1_scalar[e])
-                w_words = keep.tile([P, 512], U32, name=f"w1_words{e}{g}", align_bytes=64)
-                w_scales = keep.tile([P, 512], U8, name=f"w1_scales{e}{g}", align_bytes=64)
+        def slots_of(e):
+            return offsets[:, e * C // 16:(e + 1) * C // 16]
+
+        for step in "x0 q0 x1 q1 G0 I00 Q00 G1 I01 M000 M001 H00 Q01 M010 M011 H01 J00 R000 R001 J01 R010 R011 Y00 Y01 Y02 I10 Q10 I11 M100 M101 H10 Q11 M110 M111 H11 S00 S01 J10 R100 R101 J11 R110 R111 S02 Y10 Y11 Y12 S10 S11 S12".split():
+            kind, a = step[0], [int(ch) for ch in step[1:]]
+            if kind == "x":
+                lo, hi = x_cuts[a[0]]
+                grouped = x_grouped[:, lo:hi, :]
+                if x_shares[a[0]]:
+                    interleave(nc.scalar.copy, grouped, x_raw[a[0]], 0, x_shares[a[0]])
+                if x_shares[a[0]] < hi - lo:
+                    interleave(nc.vector.tensor_copy, grouped, x_raw[a[0]], x_shares[a[0]], hi - lo)
+            elif kind == "q":
+                lo, hi = x_cuts[a[0]]
                 nc.vector.quantize_mx(
-                    out=w_words[:].bitcast(FP8X4), scales=w_scales[:],
-                    in_=w_grouped[:].rearrange("p t m j -> p (t m j)"),
+                    out=x_words[:, lo:hi].bitcast(FP8X4), scales=x_scales[:, lo:hi],
+                    in_=x_grouped[:, lo:hi, :].rearrange("p n t -> p (n t)"),
                 )
-                for s in range(C // HALF):
-                    cols = slice(s * HALF, (s + 1) * HALF)
-                    bank = hpsum.tile([P, PACK, HALF], F32, name="h_bank")
-                    for t in range(PACK):
-                        chan = slice(t * P, (t + 1) * P)
-                        nc.tensor.matmul_mx(
-                            out=bank[:, t, :],
-                            lhsT=w_words[:, chan].bitcast(FP8X4), lhsT_scale=w_scales[:, chan],
-                            rhs=g_words[:, cols].bitcast(FP8X4), rhs_scale=g_scales[:, cols],
-                            start=True, stop=True,
-                        )
-                    h_grouped = keep.tile([P, HALF, PACK], BF16, name=f"h_grouped{e}{g}{s}", align_bytes=64)
-                    nc.scalar.activation(out=h_grouped[:], in_=bank[:].rearrange("p t n -> p n t"), func=RELU)
-                    nc.vector.quantize_mx(
-                        out=h_words[:, g, cols].bitcast(FP8X4), scales=h_scales[:, g, cols],
-                        in_=h_grouped[:].rearrange("p n t -> p (n t)"),
+            elif kind == "G":
+                e = a[0]
+                nc.vector.tensor_copy(out=g_words[e][:], in_=x_words[:].indirect(slots_of(e)))
+                nc.vector.tensor_copy(out=g_scales[e][:], in_=x_scales[:].indirect(slots_of(e)))
+            elif kind == "I":
+                e, g = a
+                w_grouped = keep.tile([P, PACK, P, PACK], BF16, name=f"w1_grouped{e}{g}", align_bytes=64)
+                share = w1_shares[e][g]
+                if share:
+                    interleave_permuted(nc.scalar.copy, w_grouped, w1_raw[e, g], 0, share)
+                if share < P:
+                    interleave_permuted(nc.vector.tensor_copy, w_grouped, w1_raw[e, g], share, P)
+                grouped1[e, g] = w_grouped
+                issue_through(ring_loads.index(f"A{e}{g}") + 3)
+            elif kind == "Q":
+                e, g = a
+                words1[e, g] = keep.tile([P, 512], U32, name=f"w1_words{e}{g}", align_bytes=64)
+                scales1[e, g] = keep.tile([P, 512], U8, name=f"w1_scales{e}{g}", align_bytes=64)
+                nc.vector.quantize_mx(
+                    out=words1[e, g][:].bitcast(FP8X4), scales=scales1[e, g][:],
+                    in_=grouped1[e, g][:].rearrange("p t m j -> p (t m j)"),
+                )
+            elif kind == "M":
+                e, g, s = a
+                if (e, g) not in h_grouped:
+                    h_grouped[e, g] = keep.tile([P, C, PACK], BF16, name=f"h_grouped{e}{g}", align_bytes=64)
+                cols = slice(s * HALF, (s + 1) * HALF)
+                bank = hpsum.tile([P, PACK, HALF], F32, name="h_bank")
+                for t in range(PACK):
+                    chan = slice(t * P, (t + 1) * P)
+                    nc.tensor.matmul_mx(
+                        out=bank[:, t, :],
+                        lhsT=words1[e, g][:, chan].bitcast(FP8X4), lhsT_scale=scales1[e, g][:, chan],
+                        rhs=g_words[e][:, cols].bitcast(FP8X4), rhs_scale=g_scales[e][:, cols],
+                        start=True, stop=True,
                     )
-
-            w2_words = keep.tile([P, HPASS, N], U32, name=f"w2_words{e}", align_bytes=64)
-            w2_scales = keep.tile([P, HPASS, N], U8, name=f"w2_scales{e}", align_bytes=64)
-            for g in range(HPASS):
+                src = bank[:].rearrange("p t n -> p n t")
+                if h_engines[e][2 * g + s] == "S":
+                    nc.scalar.activation(out=h_grouped[e, g][:, cols, :], in_=src, func=RELU)
+                else:
+                    nc.vector.tensor_scalar_max(out=h_grouped[e, g][:, cols, :], in0=src, scalar1=0.0)
+            elif kind == "H":
+                e, g = a
+                nc.vector.quantize_mx(
+                    out=h_words[e][:, g, :].bitcast(FP8X4), scales=h_scales[e][:, g, :],
+                    in_=h_grouped[e, g][:].rearrange("p n t -> p (n t)"),
+                )
+            elif kind == "J":
+                e, g = a
                 w_grouped = keep.tile([P, N, PACK], BF16, name=f"w2_grouped{e}{g}", align_bytes=64)
-                interleave(nc, w_grouped, w2_raw[e, g], N, w2_scalar[e])
-                for lo, hi in ((0, 256), (256, 384)):
-                    nc.vector.quantize_mx(
-                        out=w2_words[:, g, lo:hi].bitcast(FP8X4), scales=w2_scales[:, g, lo:hi],
-                        in_=w_grouped[:, lo:hi, :].rearrange("p n t -> p (n t)"),
-                    )
-            for b in range(NB):
+                share = w2_shares[e][g]
+                if share:
+                    interleave(nc.scalar.copy, w_grouped, w2_raw[e, g], 0, share)
+                if share < N:
+                    interleave(nc.vector.tensor_copy, w_grouped, w2_raw[e, g], share, N)
+                grouped2[e, g] = w_grouped
+                issue_through(ring_loads.index(f"B{e}{g}") + 3)
+            elif kind == "R":
+                e, g, part = a
+                lo, hi = ((0, 256), (256, 384))[part]
+                nc.vector.quantize_mx(
+                    out=words2[e][:, g, lo:hi].bitcast(FP8X4), scales=scales2[e][:, g, lo:hi],
+                    in_=grouped2[e, g][:, lo:hi, :].rearrange("p n t -> p (n t)"),
+                )
+            elif kind == "Y":
+                e, b = a
                 feat = slice(b * P, (b + 1) * P)
                 bank = ypsum.tile([P, C], F32, name="y_bank")
                 for g in range(HPASS):
                     nc.tensor.matmul_mx(
                         out=bank[:],
-                        lhsT=w2_words[:, g, feat].bitcast(FP8X4), lhsT_scale=w2_scales[:, g, feat],
-                        rhs=h_words[:, g, :].bitcast(FP8X4), rhs_scale=h_scales[:, g, :],
+                        lhsT=words2[e][:, g, feat].bitcast(FP8X4), lhsT_scale=scales2[e][:, g, feat],
+                        rhs=h_words[e][:, g, :].bitcast(FP8X4), rhs_scale=h_scales[e][:, g, :],
                         start=(g == 0), stop=(g == HPASS - 1),
                     )
                 y = keep.tile([P, C], F32, name=f"y{e}{b}")
-                nc.vector.tensor_tensor(y[:], bank[:], gate_sb[:, e * C:(e + 1) * C], MULT)
-                nc.vector.tensor_copy(windows[b][:].indirect(columns), y[:])
-                if e == E - 1:
-                    nc.sync.dma_start(out=out[feat, :], in_=windows[b][:])
+                on[y_engines[e][b]](out=y[:], in_=bank[:])
+                sums[e, b] = y
+            else:
+                e, b = a
+                nc.vector.tensor_tensor(windows[b][:].indirect(slots_of(e)), sums[e, b][:], gate_sb[:, e * C:(e + 1) * C], MULT)
+                if (1 - e, b) in done:
+                    nc.sync.dma_start(out=out[b * P:(b + 1) * P, :], in_=windows[b][:])
+                done.add((e, b))

@@ -41,7 +41,9 @@ def tile_routed_moe_kernel(tc, xT, w1, w2, gate, offs, out):
     nc = tc.nc
     with ExitStack() as ctx:
         keep = ctx.enter_context(tc.tile_pool(name="keep", bufs=1))
-        ring = ctx.enter_context(tc.tile_pool(name="ring", bufs=3))
+        ring = ctx.enter_context(tc.tile_pool(name="ring", bufs=5))
+        gring = ctx.enter_context(tc.tile_pool(name="gring", bufs=2))
+        yring = ctx.enter_context(tc.tile_pool(name="yring", bufs=2))
         hpsum = ctx.enter_context(tc.psum_pool(name="hpsum", bufs=4))
         ypsum = ctx.enter_context(tc.psum_pool(name="ypsum", bufs=4))
         on = {"S": nc.scalar.copy, "V": nc.vector.tensor_copy}
@@ -50,7 +52,7 @@ def tile_routed_moe_kernel(tc, xT, w1, w2, gate, offs, out):
         x_cuts = ((0, 512), (512, 768))
         x_raw, w1_raw, w2_raw = {}, {}, {}
         gate_sb = keep.tile([P, SLOTS], F32, name="gate_sb")
-        loads = ["X0","o","X1","A00","A01","g","B00","B01","A10","A11","B10","B11"]
+        loads = ["X1","o","X0","A00","A01","B00","B01","A10","g","A11","B10","B11"]
         ring_loads = [name for name in loads if name[0] in "AB"]
         waiting = list(loads)
 
@@ -81,7 +83,7 @@ def tile_routed_moe_kernel(tc, xT, w1, w2, gate, offs, out):
                 while ring_loads[k] in waiting:
                     issue(waiting.pop(0))
 
-        while waiting and (waiting[0] not in ring_loads or ring_loads.index(waiting[0]) < 3):
+        while waiting and (waiting[0] not in ring_loads or ring_loads.index(waiting[0]) < 5):
             issue(waiting.pop(0))
 
         windows = []
@@ -94,11 +96,11 @@ def tile_routed_moe_kernel(tc, xT, w1, w2, gate, offs, out):
         x_scales = keep.tile([P, T], U8, name="x_scales", align_bytes=64)
         nc.gpsimd.memset(x_scales[:], 0)
         x_grouped = keep.tile([P, T, PACK], BF16, name="x_grouped", align_bytes=64)
-        x_shares = [104,32]
-        w1_shares = [[128,128],[128,128]]
-        w2_shares = [[384,128],[128,128]]
-        h_engines = ["SVSV","SSSS"]
-        y_engines = ["VVS","SSS"]
+        x_shares = [168,84]
+        w1_shares = [[96,88],[120,128]]
+        w2_shares = [[0,128],[256,128]]
+        h_engines = ["SSSS","SVSS"]
+        y_engines = ["VSS","SSS"]
         words1, scales1, grouped1, h_grouped, grouped2, sums = {}, {}, {}, {}, {}, {}
         g_words, g_scales, h_words, h_scales, words2, scales2 = {}, {}, {}, {}, {}, {}
         done = set()
@@ -113,7 +115,7 @@ def tile_routed_moe_kernel(tc, xT, w1, w2, gate, offs, out):
         def slots_of(e):
             return offsets[:, e * C // 16:(e + 1) * C // 16]
 
-        for step in "x0 q0 x1 q1 G0 I00 Q00 G1 I01 M000 M001 H00 Q01 M010 M011 H01 J00 R000 R001 J01 R010 R011 Y00 Y01 Y02 I10 Q10 I11 M100 M101 H10 Q11 M110 M111 H11 S00 S01 J10 R100 R101 J11 R110 R111 S02 Y10 Y11 Y12 S10 S11 S12".split():
+        for step in "x1 q1 x0 q0 G0 I00 Q00 M001 I01 G1 Q01 M000 M010 H00 J00 M011 R000 R001 J01 H01 R010 R011 Y00 S00 Y01 Y02 I10 Q10 M100 M101 H10 I11 S01 Q11 M111 M110 H11 J10 R100 J11 R111 R110 R101 S02 Y10 S10 Y11 S11 Y12 S12".split():
             kind, a = step[0], [int(ch) for ch in step[1:]]
             if kind == "x":
                 lo, hi = x_cuts[a[0]]
@@ -134,14 +136,14 @@ def tile_routed_moe_kernel(tc, xT, w1, w2, gate, offs, out):
                 nc.vector.tensor_copy(out=g_scales[e][:], in_=x_scales[:].indirect(slots_of(e)))
             elif kind == "I":
                 e, g = a
-                w_grouped = keep.tile([P, PACK, P, PACK], BF16, name=f"w1_grouped{e}{g}", align_bytes=64)
+                w_grouped = gring.tile([P, PACK, P, PACK], BF16, name="w_grouped", align_bytes=64)
                 share = w1_shares[e][g]
                 if share:
                     interleave_permuted(nc.scalar.copy, w_grouped, w1_raw[e, g], 0, share)
                 if share < P:
                     interleave_permuted(nc.vector.tensor_copy, w_grouped, w1_raw[e, g], share, P)
                 grouped1[e, g] = w_grouped
-                issue_through(ring_loads.index(f"A{e}{g}") + 3)
+                issue_through(ring_loads.index(f"A{e}{g}") + 5)
             elif kind == "Q":
                 e, g = a
                 words1[e, g] = keep.tile([P, 512], U32, name=f"w1_words{e}{g}", align_bytes=64)
@@ -177,14 +179,14 @@ def tile_routed_moe_kernel(tc, xT, w1, w2, gate, offs, out):
                 )
             elif kind == "J":
                 e, g = a
-                w_grouped = keep.tile([P, N, PACK], BF16, name=f"w2_grouped{e}{g}", align_bytes=64)
+                w_grouped = gring.tile([P, N, PACK], BF16, name="w_grouped", align_bytes=64)
                 share = w2_shares[e][g]
                 if share:
                     interleave(nc.scalar.copy, w_grouped, w2_raw[e, g], 0, share)
                 if share < N:
                     interleave(nc.vector.tensor_copy, w_grouped, w2_raw[e, g], share, N)
                 grouped2[e, g] = w_grouped
-                issue_through(ring_loads.index(f"B{e}{g}") + 3)
+                issue_through(ring_loads.index(f"B{e}{g}") + 5)
             elif kind == "R":
                 e, g, part = a
                 lo, hi = ((0, 256), (256, 384))[part]
@@ -203,7 +205,7 @@ def tile_routed_moe_kernel(tc, xT, w1, w2, gate, offs, out):
                         rhs=h_words[e][:, g, :].bitcast(FP8X4), rhs_scale=h_scales[e][:, g, :],
                         start=(g == 0), stop=(g == HPASS - 1),
                     )
-                y = keep.tile([P, C], F32, name=f"y{e}{b}")
+                y = yring.tile([P, C], F32, name="y")
                 on[y_engines[e][b]](out=y[:], in_=bank[:])
                 sums[e, b] = y
             else:

@@ -52,17 +52,16 @@ def tile_routed_moe_kernel(tc, xT, w1, w2, gate, offs, out):
         x_cuts = ((0, 512), (512, 768))
         x_raw, w1_raw, w2_raw = {}, {}, {}
         gate_sb = keep.tile([P, SLOTS], F32, name="gate_sb")
-        loads = ["X1","o","X0","A00","A01","B00","B01","A10","g","A11","B10","B11"]
+        loads = ["X0","o","A00","A01","B00","B01","A10","g","A11","B10","B11"]
         ring_loads = [name for name in loads if name[0] in "AB"]
         waiting = list(loads)
 
         def issue(name):
             if name[0] == "X":
-                i = int(name[1])
-                lo, hi = x_cuts[i]
-                raw = keep.tile([P, PACK, hi - lo], F32, name=f"x_raw{i}")
-                nc.sync.dma_start(out=raw[:], in_=x_view[:, :, lo:hi])
-                x_raw[i] = raw
+                raw = keep.tile([P, PACK, T], F32, name="x_raw_all")
+                nc.sync.dma_start(out=raw[:], in_=x_view)
+                for i, (lo, hi) in enumerate(x_cuts):
+                    x_raw[i] = raw[:, :, lo:hi]
             elif name == "o":
                 nc.sync.dma_start(offsets[:], offs)
             elif name == "g":
@@ -106,16 +105,21 @@ def tile_routed_moe_kernel(tc, xT, w1, w2, gate, offs, out):
         done = set()
         for e in range(E):
             for table, shape, dtype, label in (
-                (g_words, [P, C], U32, "g_words"), (g_scales, [P, C], U8, "g_scales"),
                 (h_words, [P, HPASS, C], U32, "h_words"), (h_scales, [P, HPASS, C], U8, "h_scales"),
                 (words2, [P, HPASS, N], U32, "w2_words"), (scales2, [P, HPASS, N], U8, "w2_scales"),
             ):
                 table[e] = keep.tile(shape, dtype, name=f"{label}{e}", align_bytes=64)
 
+        all_words = keep.tile([P, SLOTS], U32, name="all_words", align_bytes=64)
+        all_scales = keep.tile([P, SLOTS], U8, name="all_scales", align_bytes=64)
+        for e in range(E):
+            g_words[e] = all_words[:, e * C:(e + 1) * C]
+            g_scales[e] = all_scales[:, e * C:(e + 1) * C]
+
         def slots_of(e):
             return offsets[:, e * C // 16:(e + 1) * C // 16]
 
-        for step in "x1 q1 x0 q0 G0 I00 Q00 M001 I01 G1 Q01 M000 M010 H00 J00 M011 R000 R001 J01 H01 R010 R011 Y00 S00 Y01 Y02 I10 Q10 M100 M101 H10 I11 S01 Q11 M111 M110 H11 J10 R100 J11 R111 R110 R101 S02 Y10 S10 Y11 S11 Y12 S12".split():
+        for step in "x1 q1 x0 q0 G I00 Q00 M001 I01 Q01 M000 M010 H00 J00 M011 R000 R001 J01 H01 R010 R011 Y00 S00 Y01 Y02 I10 Q10 M100 M101 H10 I11 S01 Q11 M111 M110 H11 J10 R100 J11 R111 R110 R101 S02 Y10 S10 Y11 S11 Y12 S12".split():
             kind, a = step[0], [int(ch) for ch in step[1:]]
             if kind == "x":
                 lo, hi = x_cuts[a[0]]
@@ -131,9 +135,8 @@ def tile_routed_moe_kernel(tc, xT, w1, w2, gate, offs, out):
                     in_=x_grouped[:, lo:hi, :].rearrange("p n t -> p (n t)"),
                 )
             elif kind == "G":
-                e = a[0]
-                nc.vector.tensor_copy(out=g_words[e][:], in_=x_words[:].indirect(slots_of(e)))
-                nc.vector.tensor_copy(out=g_scales[e][:], in_=x_scales[:].indirect(slots_of(e)))
+                nc.vector.tensor_copy(out=all_words[:], in_=x_words[:].indirect(offsets[:]))
+                nc.vector.tensor_copy(out=all_scales[:], in_=x_scales[:].indirect(offsets[:]))
             elif kind == "I":
                 e, g = a
                 w_grouped = gring.tile([P, PACK, P, PACK], BF16, name="w_grouped", align_bytes=64)

@@ -6,8 +6,9 @@ K, T, E, C, H, N = 512, 768, 2, 256, 1024, 384
 SLOTS = E * C
 P = 128
 PACK = 4
-HPASS = H // 512
-NB = N // P
+PASS = P * PACK
+PASSES_H = H // PASS
+BLOCKS_N = N // P
 HALF = C // 2
 
 F32 = mybir.dt.float32
@@ -20,200 +21,244 @@ RELU = mybir.ActivationFunctionType.Relu
 MULT = mybir.AluOpType.mult
 
 FLOPS = 2 * SLOTS * (K * H + H * N)
-BYTES = 4 * (K * T + E * K * H + E * H * N + SLOTS + N * T) + 2 * SLOTS
+BYTES = 4 * (K * T + E * K * H + E * H * N + N * T + SLOTS) + 2 * SLOTS
+
+TOKEN_CUTS = ((512, 768), (0, 512))
+
+WEIGHTS = (("w1", 0, 0), ("w1", 0, 1), ("w2", 0, 0), ("w2", 0, 1), ("w1", 1, 0), ("w1", 1, 1), ("w2", 1, 0), ("w2", 1, 1))
+RAW_BUFFERS = 5
+
+SCALAR_TOKENS = (84, 168)
+SCALAR_W1 = {(0, 0): 4 * 96, (0, 1): 4 * 88, (1, 0): 4 * 120, (1, 1): 4 * 128}
+SCALAR_W2 = {(0, 0): 0, (0, 1): 128, (1, 0): 256, (1, 1): 128}
 
 
-def interleave(copy, grouped, raw, lo, hi):
+def group(copy, grouped, raw, lo, hi):
     copy(
         out=grouped[:, lo:hi, :].rearrange("p (c i) t -> p c t i", i=4),
         in_=raw[:, :, lo:hi].rearrange("p t (c i) -> p c t i", i=4),
     )
 
 
-def interleave_permuted(copy, grouped, raw, lo, hi):
+def group_w1(copy, grouped, raw, lo, hi):
     copy(
-        out=grouped[:, :, lo:hi, :].rearrange("p t m j -> p m j t"),
-        in_=raw[:, :, 4 * lo:4 * hi].rearrange("p j (m t) -> p m j t", t=4),
+        out=grouped[:, :, lo // 4:hi // 4, :].rearrange("p t m j -> p m j t"),
+        in_=raw[:, :, lo:hi].rearrange("p j (m t) -> p m j t", t=4),
     )
+
+
+def share(nc, how, grouped, raw, width, scalar_columns):
+    if scalar_columns > 0:
+        how(nc.scalar.copy, grouped, raw, 0, scalar_columns)
+    if scalar_columns < width:
+        how(nc.vector.tensor_copy, grouped, raw, scalar_columns, width)
 
 
 def tile_routed_moe_kernel(tc, xT, w1, w2, gate, offs, out):
     nc = tc.nc
     with ExitStack() as ctx:
         keep = ctx.enter_context(tc.tile_pool(name="keep", bufs=1))
-        ring = ctx.enter_context(tc.tile_pool(name="ring", bufs=5))
-        gring = ctx.enter_context(tc.tile_pool(name="gring", bufs=2))
-        yring = ctx.enter_context(tc.tile_pool(name="yring", bufs=2))
-        hpsum = ctx.enter_context(tc.psum_pool(name="hpsum", bufs=4))
-        ypsum = ctx.enter_context(tc.psum_pool(name="ypsum", bufs=4))
-        on = {"S": nc.scalar.copy, "V": nc.vector.tensor_copy}
+        raw_pool = ctx.enter_context(tc.tile_pool(name="raw_pool", bufs=RAW_BUFFERS))
+        grouped_pool = ctx.enter_context(tc.tile_pool(name="grouped_pool", bufs=2))
+        first_sums = ctx.enter_context(tc.tile_pool(name="first_sums", bufs=1))
+        h_psum = ctx.enter_context(tc.psum_pool(name="h_psum", bufs=4))
+        y_psum = ctx.enter_context(tc.psum_pool(name="y_psum", bufs=4))
+
         offsets = keep.tile([P, SLOTS // 16], U16, name="offsets")
-        x_view = xT.rearrange("(p t) n -> p t n", t=PACK)
-        x_cuts = ((0, 512), (512, 768))
-        x_raw, w1_raw, w2_raw = {}, {}, {}
-        gate_sb = keep.tile([P, SLOTS], F32, name="gate_sb")
-        loads = ["X0","o","A00","A01","B00","B01","A10","g","A11","B10","B11"]
-        ring_loads = [name for name in loads if name[0] in "AB"]
-        waiting = list(loads)
-
-        def issue(name):
-            if name[0] == "X":
-                raw = keep.tile([P, PACK, T], F32, name="x_raw_all")
-                nc.sync.dma_start(out=raw[:], in_=x_view)
-                for i, (lo, hi) in enumerate(x_cuts):
-                    x_raw[i] = raw[:, :, lo:hi]
-            elif name == "o":
+        token_raw = []
+        for i, (lo, hi) in enumerate(TOKEN_CUTS):
+            raw = keep.tile([P, PACK, hi - lo], F32, name=f"token_raw{i}")
+            nc.sync.dma_start(out=raw[:], in_=xT.rearrange("(p t) n -> p t n", t=PACK)[:, :, lo:hi])
+            token_raw.append(raw)
+            if i == 0:
                 nc.sync.dma_start(offsets[:], offs)
-            elif name == "g":
-                nc.sync.dma_start(out=gate_sb[:], in_=gate[0:P, :])
-            elif name[0] == "A":
-                e, g = int(name[1]), int(name[2])
-                raw = ring.tile([P, PACK, 512], F32, name="w_raw")
-                nc.sync.dma_start(out=raw[:], in_=w1[e].rearrange("(p j) c -> p j c", j=PACK)[:, :, g * 512:(g + 1) * 512])
-                w1_raw[e, g] = raw
+
+        weight_raw = {}
+
+        def load_weights(number):
+            if number >= len(WEIGHTS):
+                return
+            matrix, e, g = WEIGHTS[number]
+            if matrix == "w1":
+                rows = w1[e, :, g * PASS:(g + 1) * PASS]
             else:
-                e, g = int(name[1]), int(name[2])
-                raw = ring.tile([P, PACK, N], F32, name="w_raw")
-                nc.sync.dma_start(out=raw[:], in_=w2[e, g * 512:(g + 1) * 512, :].rearrange("(p t) n -> p t n", t=PACK))
-                w2_raw[e, g] = raw
+                rows = w2[e, g * PASS:(g + 1) * PASS, :]
+            raw = raw_pool.tile([P, PACK, rows.shape[1]], F32, name="weight_raw")
+            nc.sync.dma_start(out=raw[:], in_=rows.rearrange("(p j) c -> p j c", j=PACK))
+            weight_raw[WEIGHTS[number]] = raw
 
-        def issue_through(k):
-            if k < len(ring_loads):
-                while ring_loads[k] in waiting:
-                    issue(waiting.pop(0))
-
-        while waiting and (waiting[0] not in ring_loads or ring_loads.index(waiting[0]) < 5):
-            issue(waiting.pop(0))
+        for number in range(RAW_BUFFERS):
+            load_weights(number)
+        gate_sb = keep.tile([P, SLOTS], F32, name="gate_sb")
+        nc.sync.dma_start(out=gate_sb[:], in_=gate[0:P, :])
 
         windows = []
-        for b in range(NB):
+        for b in range(BLOCKS_N):
             window = keep.tile([P, T], F32, name=f"window{b}")
             nc.vector.memset(window[:], 0.0)
             windows.append(window)
 
-        x_words = keep.tile([P, T], U32, name="x_words", align_bytes=64)
-        x_scales = keep.tile([P, T], U8, name="x_scales", align_bytes=64)
-        nc.gpsimd.memset(x_scales[:], 0)
-        x_grouped = keep.tile([P, T, PACK], BF16, name="x_grouped", align_bytes=64)
-        x_shares = [168,84]
-        w1_shares = [[96,88],[120,128]]
-        w2_shares = [[0,128],[256,128]]
-        h_engines = ["SSSS","SVSS"]
-        y_engines = ["VSS","SSS"]
-        words1, scales1, grouped1, h_grouped, grouped2, sums = {}, {}, {}, {}, {}, {}
-        g_words, g_scales, h_words, h_scales, words2, scales2 = {}, {}, {}, {}, {}, {}
-        done = set()
+        token_words = keep.tile([P, T], U32, name="token_words", align_bytes=64)
+        token_scales = keep.tile([P, T], U8, name="token_scales", align_bytes=64)
+        nc.gpsimd.memset(token_scales[:], 0)
+        token_grouped = keep.tile([P, T, PACK], BF16, name="token_grouped", align_bytes=64)
+        for i, (lo, hi) in enumerate(TOKEN_CUTS):
+            grouped = token_grouped[:, lo:hi, :]
+            share(nc, group, grouped, token_raw[i], hi - lo, SCALAR_TOKENS[i])
+            nc.vector.quantize_mx(
+                out=token_words[:, lo:hi].bitcast(FP8X4),
+                scales=token_scales[:, lo:hi],
+                in_=grouped.rearrange("p n t -> p (n t)"),
+            )
+
+        slot_words = keep.tile([P, SLOTS], U32, name="slot_words", align_bytes=64)
+        slot_scales = keep.tile([P, SLOTS], U8, name="slot_scales", align_bytes=64)
+        nc.vector.tensor_copy(out=slot_words[:], in_=token_words[:].indirect(offsets[:]))
+        nc.vector.tensor_copy(out=slot_scales[:], in_=token_scales[:].indirect(offsets[:]))
+
+        grouped_of = {}
+        w1_words, w1_scales, w2_words, w2_scales = {}, {}, {}, {}
+        h_grouped, h_words, h_scales = {}, {}, {}
+        y_banks, sums = {}, {}
         for e in range(E):
-            for table, shape, dtype, label in (
-                (h_words, [P, HPASS, C], U32, "h_words"), (h_scales, [P, HPASS, C], U8, "h_scales"),
-                (words2, [P, HPASS, N], U32, "w2_words"), (scales2, [P, HPASS, N], U8, "w2_scales"),
-            ):
-                table[e] = keep.tile(shape, dtype, name=f"{label}{e}", align_bytes=64)
+            h_words[e] = keep.tile([P, PASSES_H, C], U32, name=f"h_words{e}", align_bytes=64)
+            h_scales[e] = keep.tile([P, PASSES_H, C], U8, name=f"h_scales{e}", align_bytes=64)
+            w2_words[e] = keep.tile([P, PASSES_H, N], U32, name=f"w2_words{e}", align_bytes=64)
+            w2_scales[e] = keep.tile([P, PASSES_H, N], U8, name=f"w2_scales{e}", align_bytes=64)
+            for g in range(PASSES_H):
+                w1_words[e, g] = keep.tile([P, PASS], U32, name=f"w1_words{e}{g}", align_bytes=64)
+                w1_scales[e, g] = keep.tile([P, PASS], U8, name=f"w1_scales{e}{g}", align_bytes=64)
+                h_grouped[e, g] = keep.tile([P, C, PACK], BF16, name=f"h_grouped{e}{g}", align_bytes=64)
 
-        all_words = keep.tile([P, SLOTS], U32, name="all_words", align_bytes=64)
-        all_scales = keep.tile([P, SLOTS], U8, name="all_scales", align_bytes=64)
-        for e in range(E):
-            g_words[e] = all_words[:, e * C:(e + 1) * C]
-            g_scales[e] = all_scales[:, e * C:(e + 1) * C]
-
-        def slots_of(e):
-            return offsets[:, e * C // 16:(e + 1) * C // 16]
-
-        for step in "x1 q1 x0 q0 G I00 Q00 M001 I01 Q01 M000 M010 H00 J00 M011 R000 R001 J01 H01 R010 R011 Y00 S00 Y01 Y02 I10 Q10 M100 M101 H10 I11 S01 Q11 M111 M110 H11 J10 R100 J11 R111 R110 R101 S02 Y10 S10 Y11 S11 Y12 S12".split():
-            kind, a = step[0], [int(ch) for ch in step[1:]]
-            if kind == "x":
-                lo, hi = x_cuts[a[0]]
-                grouped = x_grouped[:, lo:hi, :]
-                if x_shares[a[0]]:
-                    interleave(nc.scalar.copy, grouped, x_raw[a[0]], 0, x_shares[a[0]])
-                if x_shares[a[0]] < hi - lo:
-                    interleave(nc.vector.tensor_copy, grouped, x_raw[a[0]], x_shares[a[0]], hi - lo)
-            elif kind == "q":
-                lo, hi = x_cuts[a[0]]
-                nc.vector.quantize_mx(
-                    out=x_words[:, lo:hi].bitcast(FP8X4), scales=x_scales[:, lo:hi],
-                    in_=x_grouped[:, lo:hi, :].rearrange("p n t -> p (n t)"),
-                )
-            elif kind == "G":
-                nc.vector.tensor_copy(out=all_words[:], in_=x_words[:].indirect(offsets[:]))
-                nc.vector.tensor_copy(out=all_scales[:], in_=x_scales[:].indirect(offsets[:]))
-            elif kind == "I":
-                e, g = a
-                w_grouped = gring.tile([P, PACK, P, PACK], BF16, name="w_grouped", align_bytes=64)
-                share = w1_shares[e][g]
-                if share:
-                    interleave_permuted(nc.scalar.copy, w_grouped, w1_raw[e, g], 0, share)
-                if share < P:
-                    interleave_permuted(nc.vector.tensor_copy, w_grouped, w1_raw[e, g], share, P)
-                grouped1[e, g] = w_grouped
-                issue_through(ring_loads.index(f"A{e}{g}") + 5)
-            elif kind == "Q":
-                e, g = a
-                words1[e, g] = keep.tile([P, 512], U32, name=f"w1_words{e}{g}", align_bytes=64)
-                scales1[e, g] = keep.tile([P, 512], U8, name=f"w1_scales{e}{g}", align_bytes=64)
-                nc.vector.quantize_mx(
-                    out=words1[e, g][:].bitcast(FP8X4), scales=scales1[e, g][:],
-                    in_=grouped1[e, g][:].rearrange("p t m j -> p (t m j)"),
-                )
-            elif kind == "M":
-                e, g, s = a
-                if (e, g) not in h_grouped:
-                    h_grouped[e, g] = keep.tile([P, C, PACK], BF16, name=f"h_grouped{e}{g}", align_bytes=64)
-                cols = slice(s * HALF, (s + 1) * HALF)
-                bank = hpsum.tile([P, PACK, HALF], F32, name="h_bank")
-                for t in range(PACK):
-                    chan = slice(t * P, (t + 1) * P)
-                    nc.tensor.matmul_mx(
-                        out=bank[:, t, :],
-                        lhsT=words1[e, g][:, chan].bitcast(FP8X4), lhsT_scale=scales1[e, g][:, chan],
-                        rhs=g_words[e][:, cols].bitcast(FP8X4), rhs_scale=g_scales[e][:, cols],
-                        start=True, stop=True,
-                    )
-                src = bank[:].rearrange("p t n -> p n t")
-                if h_engines[e][2 * g + s] == "S":
-                    nc.scalar.activation(out=h_grouped[e, g][:, cols, :], in_=src, func=RELU)
-                else:
-                    nc.vector.tensor_scalar_max(out=h_grouped[e, g][:, cols, :], in0=src, scalar1=0.0)
-            elif kind == "H":
-                e, g = a
-                nc.vector.quantize_mx(
-                    out=h_words[e][:, g, :].bitcast(FP8X4), scales=h_scales[e][:, g, :],
-                    in_=h_grouped[e, g][:].rearrange("p n t -> p (n t)"),
-                )
-            elif kind == "J":
-                e, g = a
-                w_grouped = gring.tile([P, N, PACK], BF16, name="w_grouped", align_bytes=64)
-                share = w2_shares[e][g]
-                if share:
-                    interleave(nc.scalar.copy, w_grouped, w2_raw[e, g], 0, share)
-                if share < N:
-                    interleave(nc.vector.tensor_copy, w_grouped, w2_raw[e, g], share, N)
-                grouped2[e, g] = w_grouped
-                issue_through(ring_loads.index(f"B{e}{g}") + 5)
-            elif kind == "R":
-                e, g, part = a
-                lo, hi = ((0, 256), (256, 384))[part]
-                nc.vector.quantize_mx(
-                    out=words2[e][:, g, lo:hi].bitcast(FP8X4), scales=scales2[e][:, g, lo:hi],
-                    in_=grouped2[e, g][:, lo:hi, :].rearrange("p n t -> p (n t)"),
-                )
-            elif kind == "Y":
-                e, b = a
-                feat = slice(b * P, (b + 1) * P)
-                bank = ypsum.tile([P, C], F32, name="y_bank")
-                for g in range(HPASS):
-                    nc.tensor.matmul_mx(
-                        out=bank[:],
-                        lhsT=words2[e][:, g, feat].bitcast(FP8X4), lhsT_scale=scales2[e][:, g, feat],
-                        rhs=h_words[e][:, g, :].bitcast(FP8X4), rhs_scale=h_scales[e][:, g, :],
-                        start=(g == 0), stop=(g == HPASS - 1),
-                    )
-                y = yring.tile([P, C], F32, name="y")
-                on[y_engines[e][b]](out=y[:], in_=bank[:])
-                sums[e, b] = y
+        def group_weights(matrix, e, g):
+            raw = weight_raw[matrix, e, g]
+            if matrix == "w1":
+                grouped = grouped_pool.tile([P, PACK, P, PACK], BF16, name="grouped", align_bytes=64)
+                share(nc, group_w1, grouped, raw, PASS, SCALAR_W1[e, g])
             else:
-                e, b = a
-                nc.vector.tensor_tensor(windows[b][:].indirect(slots_of(e)), sums[e, b][:], gate_sb[:, e * C:(e + 1) * C], MULT)
-                if (1 - e, b) in done:
-                    nc.sync.dma_start(out=out[b * P:(b + 1) * P, :], in_=windows[b][:])
-                done.add((e, b))
+                grouped = grouped_pool.tile([P, N, PACK], BF16, name="grouped", align_bytes=64)
+                share(nc, group, grouped, raw, N, SCALAR_W2[e, g])
+            grouped_of[matrix, e, g] = grouped
+            load_weights(WEIGHTS.index((matrix, e, g)) + RAW_BUFFERS)
+
+        def quantise_w1(e, g):
+            nc.vector.quantize_mx(
+                out=w1_words[e, g][:].bitcast(FP8X4),
+                scales=w1_scales[e, g][:],
+                in_=grouped_of["w1", e, g][:].rearrange("p t m j -> p (t m j)"),
+            )
+
+        def quantise_w2(e, g, lo, hi):
+            nc.vector.quantize_mx(
+                out=w2_words[e][:, g, lo:hi].bitcast(FP8X4),
+                scales=w2_scales[e][:, g, lo:hi],
+                in_=grouped_of["w2", e, g][:, lo:hi, :].rearrange("p n t -> p (n t)"),
+            )
+
+        def layer1(e, g, s):
+            slots = slice(e * C + s * HALF, e * C + (s + 1) * HALF)
+            bank = h_psum.tile([P, PACK, HALF], F32, name="h_bank")
+            for t in range(PACK):
+                chan = slice(t * P, (t + 1) * P)
+                nc.tensor.matmul_mx(
+                    out=bank[:, t, :],
+                    lhsT=w1_words[e, g][:, chan].bitcast(FP8X4),
+                    lhsT_scale=w1_scales[e, g][:, chan],
+                    rhs=slot_words[:, slots].bitcast(FP8X4),
+                    rhs_scale=slot_scales[:, slots],
+                    start=True,
+                    stop=True,
+                )
+            nc.scalar.activation(
+                out=h_grouped[e, g][:, s * HALF:(s + 1) * HALF, :],
+                in_=bank[:].rearrange("p t n -> p n t"),
+                func=RELU,
+            )
+
+        def quantise_h(e, g):
+            nc.vector.quantize_mx(
+                out=h_words[e][:, g, :].bitcast(FP8X4),
+                scales=h_scales[e][:, g, :],
+                in_=h_grouped[e, g][:].rearrange("p n t -> p (n t)"),
+            )
+
+        def layer2_pass(e, g, b):
+            feat = slice(b * P, (b + 1) * P)
+            if g == 0:
+                y_banks[e, b] = y_psum.tile([P, C], F32, name="y_bank")
+            nc.tensor.matmul_mx(
+                out=y_banks[e, b][:],
+                lhsT=w2_words[e][:, g, feat].bitcast(FP8X4),
+                lhsT_scale=w2_scales[e][:, g, feat],
+                rhs=h_words[e][:, g, :].bitcast(FP8X4),
+                rhs_scale=h_scales[e][:, g, :],
+                start=(g == 0),
+                stop=(g == PASSES_H - 1),
+            )
+
+        def finish_sums(e, b):
+            layer2_pass(e, 1, b)
+            if e == 0:
+                sums[e, b] = first_sums.tile([P, C], F32, name="sums")
+            else:
+                sums[e, b] = keep.tile([P, C], F32, name=f"last_sums{b}")
+            nc.scalar.copy(out=sums[e, b][:], in_=y_banks[e, b][:])
+
+        def scatter(e, b):
+            nc.vector.tensor_tensor(
+                windows[b][:].indirect(offsets[:, e * C // 16:(e + 1) * C // 16]),
+                sums[e, b][:],
+                gate_sb[:, e * C:(e + 1) * C],
+                MULT,
+            )
+
+        def store(b):
+            nc.sync.dma_start(out=out[b * P:(b + 1) * P, :], in_=windows[b][:])
+
+        group_weights("w1", 0, 0)
+        quantise_w1(0, 0)
+        group_weights("w1", 0, 1)
+        layer1(0, 0, 0)
+        layer1(0, 0, 1)
+        quantise_w1(0, 1)
+        quantise_h(0, 0)
+        group_weights("w2", 0, 0)
+        layer1(0, 1, 0)
+        layer1(0, 1, 1)
+        quantise_w2(0, 0, 0, 256)
+        quantise_w2(0, 0, 256, N)
+        group_weights("w2", 0, 1)
+        quantise_h(0, 1)
+        quantise_w2(0, 1, 0, 256)
+        quantise_w2(0, 1, 256, N)
+        for b in range(BLOCKS_N):
+            layer2_pass(0, 0, b)
+        finish_sums(0, 0)
+        scatter(0, 0)
+        finish_sums(0, 1)
+        finish_sums(0, 2)
+
+        group_weights("w1", 1, 0)
+        quantise_w1(1, 0)
+        layer1(1, 0, 0)
+        layer1(1, 0, 1)
+        quantise_h(1, 0)
+        group_weights("w1", 1, 1)
+        scatter(0, 1)
+        quantise_w1(1, 1)
+        layer1(1, 1, 0)
+        layer1(1, 1, 1)
+        quantise_h(1, 1)
+        group_weights("w2", 1, 0)
+        quantise_w2(1, 0, 0, 256)
+        quantise_w2(1, 0, 256, N)
+        group_weights("w2", 1, 1)
+        quantise_w2(1, 1, 0, 256)
+        quantise_w2(1, 1, 256, N)
+        scatter(0, 2)
+        for b in range(BLOCKS_N):
+            layer2_pass(1, 0, b)
+        for b in range(BLOCKS_N):
+            finish_sums(1, b)
+            scatter(1, b)
+            store(b)

from contextlib import ExitStack

import concourse.mybir as mybir

K, T, E, C, H, N = 512, 768, 2, 256, 1024, 384
SLOTS = E * C
P = 128
PACK = 4
PASS = P * PACK
PASSES_H = H // PASS
BLOCKS_N = N // P
HALF = C // 2

F32 = mybir.dt.float32
BF16 = mybir.dt.bfloat16
U32 = mybir.dt.uint32
U16 = mybir.dt.uint16
U8 = mybir.dt.uint8
FP8X4 = mybir.dt.float8_e4m3fn_x4
RELU = mybir.ActivationFunctionType.Relu
MULT = mybir.AluOpType.mult

FLOPS = 2 * SLOTS * (K * H + H * N)
BYTES = 4 * (K * T + E * K * H + E * H * N + N * T + SLOTS) + 2 * SLOTS

TOKEN_CUTS = ((512, 768), (0, 512))

WEIGHTS = (("w1", 0, 0), ("w1", 0, 1), ("w2", 0, 0), ("w2", 0, 1), ("w1", 1, 0), ("w1", 1, 1), ("w2", 1, 0), ("w2", 1, 1))
RAW_BUFFERS = 5

SCALAR_TOKENS = (84, 168)
SCALAR_W1 = {(0, 0): 4 * 96, (0, 1): 4 * 88, (1, 0): 4 * 120, (1, 1): 4 * 128}
SCALAR_W2 = {(0, 0): 0, (0, 1): 128, (1, 0): 256, (1, 1): 128}


def group(copy, grouped, raw, lo, hi):
    copy(
        out=grouped[:, lo:hi, :].rearrange("p (c i) t -> p c t i", i=4),
        in_=raw[:, :, lo:hi].rearrange("p t (c i) -> p c t i", i=4),
    )


def group_w1(copy, grouped, raw, lo, hi):
    copy(
        out=grouped[:, :, lo // 4:hi // 4, :].rearrange("p t m j -> p m j t"),
        in_=raw[:, :, lo:hi].rearrange("p j (m t) -> p m j t", t=4),
    )


def share(nc, how, grouped, raw, width, scalar_columns):
    if scalar_columns > 0:
        how(nc.scalar.copy, grouped, raw, 0, scalar_columns)
    if scalar_columns < width:
        how(nc.vector.tensor_copy, grouped, raw, scalar_columns, width)


def tile_routed_moe_kernel(tc, xT, w1, w2, gate, offs, out):
    nc = tc.nc
    with ExitStack() as ctx:
        keep = ctx.enter_context(tc.tile_pool(name="keep", bufs=1))
        raw_pool = ctx.enter_context(tc.tile_pool(name="raw_pool", bufs=RAW_BUFFERS))
        grouped_pool = ctx.enter_context(tc.tile_pool(name="grouped_pool", bufs=2))
        first_sums = ctx.enter_context(tc.tile_pool(name="first_sums", bufs=1))
        h_psum = ctx.enter_context(tc.psum_pool(name="h_psum", bufs=4))
        y_psum = ctx.enter_context(tc.psum_pool(name="y_psum", bufs=4))

        offsets = keep.tile([P, SLOTS // 16], U16, name="offsets")
        token_raw = []
        for i, (lo, hi) in enumerate(TOKEN_CUTS):
            raw = keep.tile([P, PACK, hi - lo], F32, name=f"token_raw{i}")
            nc.sync.dma_start(out=raw[:], in_=xT.rearrange("(p t) n -> p t n", t=PACK)[:, :, lo:hi])
            token_raw.append(raw)
            if i == 0:
                nc.sync.dma_start(offsets[:], offs)

        weight_raw = {}

        def load_weights(number):
            if number >= len(WEIGHTS):
                return
            matrix, e, g = WEIGHTS[number]
            if matrix == "w1":
                rows = w1[e, :, g * PASS:(g + 1) * PASS]
            else:
                rows = w2[e, g * PASS:(g + 1) * PASS, :]
            raw = raw_pool.tile([P, PACK, rows.shape[1]], F32, name="weight_raw")
            nc.sync.dma_start(out=raw[:], in_=rows.rearrange("(p j) c -> p j c", j=PACK))
            weight_raw[WEIGHTS[number]] = raw

        for number in range(RAW_BUFFERS):
            load_weights(number)
        gate_sb = keep.tile([P, SLOTS], F32, name="gate_sb")
        nc.sync.dma_start(out=gate_sb[:], in_=gate[0:P, :])

        windows = []
        for b in range(BLOCKS_N):
            window = keep.tile([P, T], F32, name=f"window{b}")
            nc.vector.memset(window[:], 0.0)
            windows.append(window)

        token_words = keep.tile([P, T], U32, name="token_words", align_bytes=64)
        token_scales = keep.tile([P, T], U8, name="token_scales", align_bytes=64)
        nc.gpsimd.memset(token_scales[:], 0)
        token_grouped = keep.tile([P, T, PACK], BF16, name="token_grouped", align_bytes=64)
        for i, (lo, hi) in enumerate(TOKEN_CUTS):
            grouped = token_grouped[:, lo:hi, :]
            share(nc, group, grouped, token_raw[i], hi - lo, SCALAR_TOKENS[i])
            nc.vector.quantize_mx(
                out=token_words[:, lo:hi].bitcast(FP8X4),
                scales=token_scales[:, lo:hi],
                in_=grouped.rearrange("p n t -> p (n t)"),
            )

        slot_words = keep.tile([P, SLOTS], U32, name="slot_words", align_bytes=64)
        slot_scales = keep.tile([P, SLOTS], U8, name="slot_scales", align_bytes=64)
        nc.vector.tensor_copy(out=slot_words[:], in_=token_words[:].indirect(offsets[:]))
        nc.vector.tensor_copy(out=slot_scales[:], in_=token_scales[:].indirect(offsets[:]))

        grouped_of = {}
        w1_words, w1_scales, w2_words, w2_scales = {}, {}, {}, {}
        h_grouped, h_words, h_scales = {}, {}, {}
        y_banks, sums = {}, {}
        for e in range(E):
            h_words[e] = keep.tile([P, PASSES_H, C], U32, name=f"h_words{e}", align_bytes=64)
            h_scales[e] = keep.tile([P, PASSES_H, C], U8, name=f"h_scales{e}", align_bytes=64)
            w2_words[e] = keep.tile([P, PASSES_H, N], U32, name=f"w2_words{e}", align_bytes=64)
            w2_scales[e] = keep.tile([P, PASSES_H, N], U8, name=f"w2_scales{e}", align_bytes=64)
            for g in range(PASSES_H):
                w1_words[e, g] = keep.tile([P, PASS], U32, name=f"w1_words{e}{g}", align_bytes=64)
                w1_scales[e, g] = keep.tile([P, PASS], U8, name=f"w1_scales{e}{g}", align_bytes=64)
                h_grouped[e, g] = keep.tile([P, C, PACK], BF16, name=f"h_grouped{e}{g}", align_bytes=64)

        def group_weights(matrix, e, g):
            raw = weight_raw[matrix, e, g]
            if matrix == "w1":
                grouped = grouped_pool.tile([P, PACK, P, PACK], BF16, name="grouped", align_bytes=64)
                share(nc, group_w1, grouped, raw, PASS, SCALAR_W1[e, g])
            else:
                grouped = grouped_pool.tile([P, N, PACK], BF16, name="grouped", align_bytes=64)
                share(nc, group, grouped, raw, N, SCALAR_W2[e, g])
            grouped_of[matrix, e, g] = grouped
            load_weights(WEIGHTS.index((matrix, e, g)) + RAW_BUFFERS)

        def quantise_w1(e, g):
            nc.vector.quantize_mx(
                out=w1_words[e, g][:].bitcast(FP8X4),
                scales=w1_scales[e, g][:],
                in_=grouped_of["w1", e, g][:].rearrange("p t m j -> p (t m j)"),
            )

        def quantise_w2(e, g, lo, hi):
            nc.vector.quantize_mx(
                out=w2_words[e][:, g, lo:hi].bitcast(FP8X4),
                scales=w2_scales[e][:, g, lo:hi],
                in_=grouped_of["w2", e, g][:, lo:hi, :].rearrange("p n t -> p (n t)"),
            )

        def layer1(e, g, s):
            slots = slice(e * C + s * HALF, e * C + (s + 1) * HALF)
            bank = h_psum.tile([P, PACK, HALF], F32, name="h_bank")
            for t in range(PACK):
                chan = slice(t * P, (t + 1) * P)
                nc.tensor.matmul_mx(
                    out=bank[:, t, :],
                    lhsT=w1_words[e, g][:, chan].bitcast(FP8X4),
                    lhsT_scale=w1_scales[e, g][:, chan],
                    rhs=slot_words[:, slots].bitcast(FP8X4),
                    rhs_scale=slot_scales[:, slots],
                    start=True,
                    stop=True,
                )
            nc.scalar.activation(
                out=h_grouped[e, g][:, s * HALF:(s + 1) * HALF, :],
                in_=bank[:].rearrange("p t n -> p n t"),
                func=RELU,
            )

        def quantise_h(e, g):
            nc.vector.quantize_mx(
                out=h_words[e][:, g, :].bitcast(FP8X4),
                scales=h_scales[e][:, g, :],
                in_=h_grouped[e, g][:].rearrange("p n t -> p (n t)"),
            )

        def layer2_pass(e, g, b):
            feat = slice(b * P, (b + 1) * P)
            if g == 0:
                y_banks[e, b] = y_psum.tile([P, C], F32, name="y_bank")
            nc.tensor.matmul_mx(
                out=y_banks[e, b][:],
                lhsT=w2_words[e][:, g, feat].bitcast(FP8X4),
                lhsT_scale=w2_scales[e][:, g, feat],
                rhs=h_words[e][:, g, :].bitcast(FP8X4),
                rhs_scale=h_scales[e][:, g, :],
                start=(g == 0),
                stop=(g == PASSES_H - 1),
            )

        def finish_sums(e, b):
            layer2_pass(e, 1, b)
            if e == 0:
                sums[e, b] = first_sums.tile([P, C], F32, name="sums")
            else:
                sums[e, b] = keep.tile([P, C], F32, name=f"last_sums{b}")
            nc.scalar.copy(out=sums[e, b][:], in_=y_banks[e, b][:])

        def scatter(e, b):
            nc.vector.tensor_tensor(
                windows[b][:].indirect(offsets[:, e * C // 16:(e + 1) * C // 16]),
                sums[e, b][:],
                gate_sb[:, e * C:(e + 1) * C],
                MULT,
            )

        def store(b):
            nc.sync.dma_start(out=out[b * P:(b + 1) * P, :], in_=windows[b][:])

        group_weights("w1", 0, 0)
        quantise_w1(0, 0)
        group_weights("w1", 0, 1)
        layer1(0, 0, 0)
        layer1(0, 0, 1)
        quantise_w1(0, 1)
        quantise_h(0, 0)
        group_weights("w2", 0, 0)
        layer1(0, 1, 0)
        layer1(0, 1, 1)
        quantise_w2(0, 0, 0, 256)
        quantise_w2(0, 0, 256, N)
        group_weights("w2", 0, 1)
        quantise_h(0, 1)
        quantise_w2(0, 1, 0, 256)
        quantise_w2(0, 1, 256, N)
        for b in range(BLOCKS_N):
            layer2_pass(0, 0, b)
        finish_sums(0, 0)
        scatter(0, 0)
        finish_sums(0, 1)
        finish_sums(0, 2)

        group_weights("w1", 1, 0)
        quantise_w1(1, 0)
        layer1(1, 0, 0)
        layer1(1, 0, 1)
        quantise_h(1, 0)
        group_weights("w1", 1, 1)
        scatter(0, 1)
        quantise_w1(1, 1)
        layer1(1, 1, 0)
        layer1(1, 1, 1)
        quantise_h(1, 1)
        group_weights("w2", 1, 0)
        quantise_w2(1, 0, 0, 256)
        quantise_w2(1, 0, 256, N)
        group_weights("w2", 1, 1)
        quantise_w2(1, 1, 0, 256)
        quantise_w2(1, 1, 256, N)
        scatter(0, 2)
        for b in range(BLOCKS_N):
            layer2_pass(1, 0, b)
        for b in range(BLOCKS_N):
            finish_sums(1, b)
            scatter(1, b)
            store(b)
